import numpy as np
import ml_dtypes


def mxq(x, axis, fmt="e4m3"):
    dtype, down = {"e4m3": (ml_dtypes.float8_e4m3fn, 7), "e5m2": (ml_dtypes.float8_e5m2, 14)}[fmt]
    v = np.moveaxis(np.asarray(x, np.float32).astype(ml_dtypes.bfloat16).astype(np.float64), axis, -1)
    blocks = v.reshape(v.shape[:-1] + (-1, 32))
    amax = np.abs(blocks).max(-1, keepdims=True)
    byte = np.maximum(np.where(amax > 0, np.frexp(amax)[1] - 1 + 127, 0) - down, 1)
    scale = np.exp2(byte - 127.0)
    codes = (blocks / scale).astype(np.float32).astype(dtype).astype(np.float64)
    return np.moveaxis((codes * scale).reshape(v.shape), -1, axis)


WIDE = False


def mx_kscale(k):
    if not WIDE:
        return np.ones(k)
    levels = np.array([10, -10, 5, -5, 0])
    if k % 512:
        return np.exp2(np.random.permutation(np.resize(levels, k // 32))).repeat(32)
    a = np.empty((k // 512, 16))
    for p in range(k // 512):
        a[p, :8] = np.random.permutation(np.resize(levels, 8))
        for g in range(8):
            far = levels[np.abs(levels - a[p, g]) >= 10]
            a[p, g + 8] = far[np.random.randint(len(far))]
    return np.exp2(a.ravel()).repeat(32)


def f64(x):
    return np.asarray(x).astype(np.float64)


def striped(idx):
    return np.tile(idx.reshape(-1, 16).T, (8, 1)).astype(np.uint16)


def unstriped(offs):
    return offs[:16].T.reshape(-1).astype(np.int64)


def striped8(idx):
    return np.concatenate([x.reshape(-1, 16).T for x in idx]).astype(np.uint16)


def runs(offs, k):
    lists = np.stack([offs[16 * r : 16 * r + 16].T.reshape(-1) for r in range(8)]).astype(np.int64)
    return lists[np.arange(k) % 512 // 64]


def pack_weight(w):
    k, n = w.shape
    w = f64(np.asarray(w, np.float32).astype(ml_dtypes.bfloat16)).reshape(k // 32, 32, n)
    amax = np.abs(w).max(1)
    byte = np.clip(np.where(amax > 0, np.frexp(amax)[1] - 1 + 127 - 7, 1), 1, 254)
    scaled = (w * np.exp2(127.0 - byte)[:, None, :]).reshape(k, n).astype(np.float32)
    words = np.ascontiguousarray(scaled.reshape(k // 512, 128, 4, n).transpose(0, 1, 3, 2)).astype(ml_dtypes.float8_e4m3fn).view(np.uint8)
    return words, np.ascontiguousarray(byte.astype(np.uint8).reshape(k // 512, 16, n))


def unpack_weight(words, scales):
    g, p, n, _ = words.shape
    vals = np.ascontiguousarray(words).view(ml_dtypes.float8_e4m3fn).astype(np.float64) * np.repeat(np.exp2(scales.astype(np.float64) - 127.0), 8, axis=1)[..., None]
    return vals.transpose(0, 1, 3, 2).reshape(g * 512, n)


def sigmoid(v):
    return 1.0 / (1.0 + np.exp(-np.maximum(v, -700.0)))


K, T, S, G, H, C = 512, 1024, 512, 2048, 512, 512


def setup_inputs():
    n = np.random.standard_normal
    s = mx_kscale(K)[:, None]
    packed_xT = pack_weight(n((K, T)) * s)
    packed_dT = pack_weight(n((K, G)) / s)
    return {
        "x_words": packed_xT[0],
        "x_scales": packed_xT[1],
        "d_words": packed_dT[0],
        "d_scales": packed_dT[1],
        "gs": (np.random.uniform(0.5, 1.5, (K, 1)) / s).astype(np.float32),
        "offs": striped(np.random.permutation(T)[:S]),
        "k1": striped8(np.random.randint(0, G, (8, H))),
        "n1": striped8(np.stack([np.random.permutation(S) for _ in range(8)])),
        "n2": striped8(np.stack([np.random.permutation(S) for _ in range(8)])),
        "cand": striped(np.random.permutation(T)[:C]),
        "n3": striped8(np.stack([np.random.permutation(S) for _ in range(8)])),
        "n4": striped8(np.stack([np.random.permutation(S) for _ in range(8)])),
    }


def reference(x_words, x_scales, d_words, d_scales, gs, offs, k1, n1, n2, cand, n3, n4):
    x_cand = unpack_weight(x_words, x_scales)[:, unstriped(cand)]
    d_k1 = unpack_weight(d_words, d_scales)[np.arange(K)[:, None], runs(k1, K)]
    xq = unpack_weight(x_words, x_scales)[:, unstriped(offs)]
    h = 0.0625 * (d_k1.T @ xq)
    z = f64(gs) * (np.maximum(h * (sigmoid(h[np.arange(H)[:, None], runs(n1, H)])), h[np.arange(H)[:, None], runs(n2, H)]))
    s = 0.0625 * ((x_cand.T @ mxq(z, 0, "e4m3")))
    ex = np.exp(s)
    return np.log(ex + ex[np.arange(C)[:, None], runs(n3, C)]) - (s[np.arange(C)[:, None], runs(n4, C)])

@@ -1,0 +1,216 @@
+from contextlib import ExitStack
+
+import concourse.mybir as mybir
+
+K, T, S, G, H, C = 512, 1024, 512, 2048, 512, 512
+P = 128
+PACK = 4
+FLOPS = 2 * K * H * S + 2 * K * C * S
+
+F32 = mybir.dt.float32
+BF16 = mybir.dt.bfloat16
+I32 = mybir.dt.int32
+U32 = mybir.dt.uint32
+U16 = mybir.dt.uint16
+U8 = mybir.dt.uint8
+FP8X4 = mybir.dt.float8_e4m3fn_x4
+ACT = mybir.ActivationFunctionType
+ALU = mybir.AluOpType
+
+
+def tile_picked_pqcgmaxlse_none_p_kernel(
+    tc, x_words, x_scales, d_words, d_scales, gs, offs, k1, n1, n2, cand, n3, n4, out
+):
+    nc = tc.nc
+    with ExitStack() as ctx:
+        lists = ctx.enter_context(tc.tile_pool(name="lists", bufs=1))
+        keep = ctx.enter_context(tc.tile_pool(name="keep", bufs=1))
+        psum = ctx.enter_context(tc.psum_pool(name="psum", bufs=1))
+
+        def load_list(name, source):
+            tile = lists.tile([P, S // 16], U16, name=name)
+            nc.sync.dma_start(tile[:], source)
+            return tile
+
+        d_table = keep.tile([P, G], U32, align_bytes=64)
+        d_bytes = keep.tile([P, G], U8, align_bytes=64)
+        x_table = keep.tile([P, T], U32, align_bytes=64)
+        x_bytes = keep.tile([P, T], U8, align_bytes=64)
+        w_scales = keep.tile([P, H], U8, align_bytes=64)
+        gain = keep.tile([P, PACK], F32)
+        warm = keep.tile([P, 8], F32)
+        warmed = keep.tile([P, 8], F32)
+
+        nc.vector.memset(d_bytes[:].bitcast(I32), 0)
+        nc.vector.memset(x_bytes[:].bitcast(I32), 0)
+        nc.vector.memset(w_scales[:].bitcast(I32), 0)
+        nc.vector.memset(warm[:], 0.0)
+
+        nc.sync.dma_start(
+            x_table[:].bitcast(I32), x_words[0].rearrange("p n r -> p (n r)").bitcast(I32)
+        )
+        offs_list = load_list("offs_list", offs)
+        k1_list = load_list("k1_list", k1)
+        nc.scalar.dma_start(d_bytes[0:P:8, :].bitcast(I32), d_scales[0].bitcast(I32))
+        for q in range(4):
+            nc.scalar.dma_start(
+                x_bytes[32 * q : 32 * q + 4, :].bitcast(I32),
+                x_scales[0, 4 * q : 4 * q + 4, :].bitcast(I32),
+            )
+        cand_list = load_list("cand_list", cand)
+        n1_list = load_list("n1_list", n1)
+        n2_list = load_list("n2_list", n2)
+        n3_list = load_list("n3_list", n3)
+        nc.sync.dma_start(
+            d_table[:].bitcast(I32), d_words[0].rearrange("p n r -> p (n r)").bitcast(I32)
+        )
+        n4_list = load_list("n4_list", n4)
+        nc.sync.dma_start(gain[:], gs.rearrange("(p t) o -> p (t o)", t=PACK))
+        nc.scalar.activation(warmed[:], warm[:], ACT.Sigmoid)
+
+        def gather(name, table, offsets, dtype, tag=None):
+            picked = keep.tile([P, S], dtype, name=name, tag=tag or name, align_bytes=64)
+            nc.vector.tensor_copy(picked[:], table[:].indirect(offsets[:]))
+            return picked
+
+        def deal(name, picked, dtype):
+            dealt = keep.tile([P, S], dtype, name=name, align_bytes=64)
+            nc.vector.tensor_copy(
+                dealt[:].rearrange("p (t m) -> p t m", t=PACK),
+                picked[:].rearrange("p (m t) -> p t m", t=PACK),
+            )
+            return dealt
+
+        xq_codes = gather("xq_codes", x_table, offs_list, U32)
+        w_bytes = deal("w_bytes", gather("w_bytes_picked", d_bytes, k1_list, U8), U8)
+        for b in range(4):
+            nc.sync.dma_start(
+                w_scales[b:P:32, :].bitcast(I32), w_bytes[8 * b : P : 32, :].bitcast(I32)
+            )
+        xq_scales = gather("xq_scales", x_bytes, offs_list, U8)
+        w_codes = deal("w_codes", gather("w_codes_picked", d_table, k1_list, U32, "picked"), U32)
+
+        h_banks = [psum.tile([P, S], F32, name=f"h_bank{t}", tag=f"bank{t}") for t in range(PACK)]
+        for t in range(PACK):
+            cols = slice(P * t, P * (t + 1))
+            nc.tensor.matmul_mx(
+                out=h_banks[t][:],
+                lhsT=w_codes[:, cols].bitcast(FP8X4),
+                lhsT_scale=w_scales[:, cols],
+                rhs=xq_codes[:].bitcast(FP8X4),
+                rhs_scale=xq_scales[:],
+                start=True,
+                stop=True,
+            )
+
+        c_codes = deal("c_codes", gather("c_codes_picked", x_table, cand_list, U32, "picked"), U32)
+        c_scales = deal("c_scales", gather("c_scales_picked", x_bytes, cand_list, U8, "picked"), U8)
+
+        half = S // 2
+        h_rows = [keep.tile([P, S], F32, name=f"h_rows{t}", align_bytes=64) for t in range(PACK)]
+        s_rows = [keep.tile([P, 2 * S], F32, name=f"s_rows{t}", align_bytes=64) for t in range(PACK)]
+        gates = [keep.tile([P, S], F32, name=f"gate{t}") for t in range(PACK)]
+        own = [keep.tile([P, S], F32, name=f"own{t}") for t in range(PACK)]
+        z_planes = [keep.tile([P, PACK, half], BF16, name=f"z_planes{u}", align_bytes=64) for u in range(2)]
+        z_grouped = [keep.tile([P, half, PACK], BF16, name=f"z_grouped{u}", align_bytes=64) for u in range(2)]
+        z_codes = [keep.tile([P, half], U32, name=f"z_codes{u}", align_bytes=64) for u in range(2)]
+        z_scales = [keep.tile([P, half], U8, name=f"z_scales{u}", align_bytes=64) for u in range(2)]
+        s_banks = {}
+
+        def places(u):
+            return slice(half * u, half * (u + 1))
+
+        def entries(u):
+            return slice(half // 16 * u, half // 16 * (u + 1))
+
+        def gate(t, u):
+            nc.scalar.activation(
+                gates[t][:, places(u)], h_rows[t][:].indirect(n1_list[:, entries(u)]), ACT.Sigmoid
+            )
+
+        def choose(t, u):
+            second = keep.tile([P, half], F32, name=f"second{t}{u}")
+            first = keep.tile([P, half], F32, name=f"first{t}{u}")
+            nc.vector.tensor_copy(second[:], h_rows[t][:].indirect(n2_list[:, entries(u)]))
+            nc.vector.tensor_tensor(first[:], h_rows[t][:, places(u)], gates[t][:, places(u)], ALU.mult)
+            nc.vector.tensor_tensor(
+                s_rows[t][:, S + half * u : S + half * (u + 1)], first[:], second[:], ALU.max
+            )
+
+        def weigh(t, u):
+            nc.scalar.activation(
+                z_planes[u][:, t, :],
+                s_rows[t][:, S + half * u : S + half * (u + 1)],
+                ACT.Copy,
+                scale=gain[:, t : t + 1],
+            )
+
+        def score(u):
+            nc.vector.quantize_mx(
+                out=z_codes[u][:].bitcast(FP8X4),
+                scales=z_scales[u][:],
+                in_=z_grouped[u][:].rearrange("p j t -> p (j t)"),
+            )
+            for t in range(PACK):
+                cols = slice(P * t, P * (t + 1))
+                bank = psum.tile([P, half], F32, name=f"s_bank{t}{u}", tag=f"bank{t + PACK * (1 - u)}")
+                nc.tensor.matmul_mx(
+                    out=bank[:],
+                    lhsT=c_codes[:, cols].bitcast(FP8X4),
+                    lhsT_scale=c_scales[:, cols],
+                    rhs=z_codes[u][:].bitcast(FP8X4),
+                    rhs_scale=z_scales[u][:],
+                    start=True,
+                    stop=True,
+                )
+                s_banks[t, u] = bank
+
+        def exp_own(t, u):
+            nc.scalar.activation(own[t][:, places(u)], s_banks[t, u][:], ACT.Exp, scale=0.0625)
+
+        for t in range(PACK):
+            nc.scalar.activation(h_rows[t][:], h_banks[t][:], ACT.Copy, scale=0.0625)
+            gate(t, 0)
+        for t in range(PACK):
+            choose(t, 0)
+            gate(t, 1)
+            weigh(t, 0)
+        nc.scalar.copy(z_grouped[0][:], z_planes[0][:].rearrange("p t j -> p j t"))
+        choose(0, 1)
+        weigh(0, 1)
+        choose(1, 1)
+        score(0)
+        exp_own(0, 0)
+        weigh(1, 1)
+        choose(2, 1)
+        weigh(2, 1)
+        choose(3, 1)
+        weigh(3, 1)
+        for t in range(PACK):
+            nc.scalar.activation(s_rows[t][:, places(0)], s_banks[t, 0][:], ACT.Copy, scale=0.0625)
+        for t in range(1, PACK):
+            exp_own(t, 0)
+        nc.vector.tensor_copy(z_grouped[1][:], z_planes[1][:].rearrange("p t j -> p j t"))
+        score(1)
+
+        sums, taken = [], []
+        for t in range(PACK):
+            nc.vector.tensor_scalar_mul(s_rows[t][:, places(1)], s_banks[t, 1][:], 0.0625)
+        for t in range(PACK):
+            other = keep.tile([P, S], F32, name=f"other{t}")
+            both = keep.tile([P, S], F32, name=f"both{t}")
+            less = keep.tile([P, S], F32, name=f"less{t}")
+            nc.scalar.activation(own[t][:, places(1)], s_rows[t][:, places(1)], ACT.Exp)
+            nc.scalar.activation(other[:], s_rows[t][:].indirect(n3_list[:]), ACT.Exp)
+            nc.vector.tensor_copy(less[:], s_rows[t][:].indirect(n4_list[:]))
+            nc.vector.tensor_tensor(both[:], own[t][:], other[:], ALU.add)
+            sums.append(both)
+            taken.append(less)
+        out_rows = out.rearrange("(p t) j -> t p j", t=PACK)
+        for t in range(PACK):
+            logs = keep.tile([P, S], F32, name=f"logs{t}")
+            result = keep.tile([P, S], F32, name=f"result{t}")
+            for cols in [slice(0, S)] if t < PACK - 1 else [places(0), places(1)]:
+                nc.scalar.activation(logs[:, cols], sums[t][:, cols], ACT.Ln)
+                nc.vector.tensor_tensor(result[:, cols], logs[:, cols], taken[t][:, cols], ALU.subtract)
+                nc.sync.dma_start(out_rows[t][:, cols], result[:, cols])

@@ -25,6 +25,7 @@ def tile_picked_pqcgmaxlse_none_p_kernel(
     with ExitStack() as ctx:
         lists = ctx.enter_context(tc.tile_pool(name="lists", bufs=1))
         keep = ctx.enter_context(tc.tile_pool(name="keep", bufs=1))
+        staging = ctx.enter_context(tc.tile_pool(name="staging", bufs=1))
         psum = ctx.enter_context(tc.psum_pool(name="psum", bufs=1))
 
         def load_list(name, source):
@@ -38,57 +39,63 @@ def tile_picked_pqcgmaxlse_none_p_kernel(
         x_bytes = keep.tile([P, T], U8, align_bytes=64)
         w_scales = keep.tile([P, H], U8, align_bytes=64)
         gain = keep.tile([P, PACK], F32)
-        warm = keep.tile([P, 8], F32)
         warmed = keep.tile([P, 8], F32)
 
-        nc.vector.memset(d_bytes[:].bitcast(I32), 0)
-        nc.vector.memset(x_bytes[:].bitcast(I32), 0)
-        nc.vector.memset(w_scales[:].bitcast(I32), 0)
-        nc.vector.memset(warm[:], 0.0)
+        rows = [keep.tile([P, 2 * S], F32, name=f"rows{t}", align_bytes=64) for t in range(PACK)]
 
-        nc.sync.dma_start(
-            x_table[:].bitcast(I32), x_words[0].rearrange("p n r -> p (n r)").bitcast(I32)
-        )
-        offs_list = load_list("offs_list", offs)
+        nc.vector.memset(d_bytes[:].bitcast(I32), 0)
+        nc.gpsimd.memset(x_bytes[:].bitcast(I32), 0)
+        nc.vector.memset(w_scales[:].bitcast(I32), 0)
+        for t in range(PACK):
+            nc.vector.memset(rows[t][:, S:], 0.0)
+
         k1_list = load_list("k1_list", k1)
-        nc.scalar.dma_start(d_bytes[0:P:8, :].bitcast(I32), d_scales[0].bitcast(I32))
+        offs_list = load_list("offs_list", offs)
+        nc.sync.dma_start(d_bytes[0:P:8, :].bitcast(I32), d_scales[0].bitcast(I32))
         for q in range(4):
-            nc.scalar.dma_start(
+            nc.sync.dma_start(
                 x_bytes[32 * q : 32 * q + 4, :].bitcast(I32),
                 x_scales[0, 4 * q : 4 * q + 4, :].bitcast(I32),
             )
         cand_list = load_list("cand_list", cand)
         n1_list = load_list("n1_list", n1)
+        nc.sync.dma_start(
+            x_table[:].bitcast(I32), x_words[0].rearrange("p n r -> p (n r)").bitcast(I32)
+        )
         n2_list = load_list("n2_list", n2)
-        n3_list = load_list("n3_list", n3)
         nc.sync.dma_start(
             d_table[:].bitcast(I32), d_words[0].rearrange("p n r -> p (n r)").bitcast(I32)
         )
-        n4_list = load_list("n4_list", n4)
         nc.sync.dma_start(gain[:], gs.rearrange("(p t) o -> p (t o)", t=PACK))
-        nc.scalar.activation(warmed[:], warm[:], ACT.Sigmoid)
+        n3_list = load_list("n3_list", n3)
+        n4_list = load_list("n4_list", n4)
+        nc.scalar.activation(warmed[:], rows[0][:, S : S + 8], ACT.Sigmoid)
 
-        def gather(name, table, offsets, dtype, tag=None):
-            picked = keep.tile([P, S], dtype, name=name, tag=tag or name, align_bytes=64)
+        def gather(picked, table, offsets):
             nc.vector.tensor_copy(picked[:], table[:].indirect(offsets[:]))
-            return picked
 
-        def deal(name, picked, dtype):
-            dealt = keep.tile([P, S], dtype, name=name, align_bytes=64)
+        def deal(dealt, picked):
             nc.vector.tensor_copy(
                 dealt[:].rearrange("p (t m) -> p t m", t=PACK),
                 picked[:].rearrange("p (m t) -> p t m", t=PACK),
             )
-            return dealt
 
-        xq_codes = gather("xq_codes", x_table, offs_list, U32)
-        w_bytes = deal("w_bytes", gather("w_bytes_picked", d_bytes, k1_list, U8), U8)
+        w_bytes_picked = keep.tile([P, H], U8)
+        w_bytes = keep.tile([P, H], U8)
+        w_codes_picked = staging.tile([P, H], U32, offset=0)
+        w_codes = keep.tile([P, H], U32, align_bytes=64)
+        xq_codes = keep.tile([P, S], U32, align_bytes=64)
+        xq_scales = keep.tile([P, S], U8, align_bytes=64)
+        gather(w_bytes_picked, d_bytes, k1_list)
+        gather(xq_scales, x_bytes, offs_list)
+        deal(w_bytes, w_bytes_picked)
         for b in range(4):
             nc.sync.dma_start(
                 w_scales[b:P:32, :].bitcast(I32), w_bytes[8 * b : P : 32, :].bitcast(I32)
             )
-        xq_scales = gather("xq_scales", x_bytes, offs_list, U8)
-        w_codes = deal("w_codes", gather("w_codes_picked", d_table, k1_list, U32, "picked"), U32)
+        gather(w_codes_picked, d_table, k1_list)
+        gather(xq_codes, x_table, offs_list)
+        deal(w_codes, w_codes_picked)
 
         h_banks = [psum.tile([P, S], F32, name=f"h_bank{t}", tag=f"bank{t}") for t in range(PACK)]
         for t in range(PACK):
@@ -103,46 +110,62 @@ def tile_picked_pqcgmaxlse_none_p_kernel(
                 stop=True,
             )
 
-        c_codes = deal("c_codes", gather("c_codes_picked", x_table, cand_list, U32, "picked"), U32)
-        c_scales = deal("c_scales", gather("c_scales_picked", x_bytes, cand_list, U8, "picked"), U8)
+        c_scales_picked = staging.tile([P, C], U8, offset=0)
+        c_codes_picked = staging.tile([P, C], U32, offset=C)
+        c_codes = keep.tile([P, C], U32, align_bytes=64)
+        c_scales = keep.tile([P, C], U8, align_bytes=64)
+        gather(c_codes_picked, x_table, cand_list)
+        gather(c_scales_picked, x_bytes, cand_list)
+        deal(c_codes, c_codes_picked)
+        deal(c_scales, c_scales_picked)
 
         half = S // 2
-        h_rows = [keep.tile([P, S], F32, name=f"h_rows{t}", align_bytes=64) for t in range(PACK)]
-        s_rows = [keep.tile([P, 2 * S], F32, name=f"s_rows{t}", align_bytes=64) for t in range(PACK)]
-        gates = [keep.tile([P, S], F32, name=f"gate{t}") for t in range(PACK)]
-        own = [keep.tile([P, S], F32, name=f"own{t}") for t in range(PACK)]
-        z_planes = [keep.tile([P, PACK, half], BF16, name=f"z_planes{u}", align_bytes=64) for u in range(2)]
+        ex_rows = [keep.tile([P, 2 * S], F32, name=f"ex_rows{t}", align_bytes=64) for t in range(PACK)]
+        ex_own = [keep.tile([P, S], F32, name=f"ex_own{t}") for t in range(PACK)]
+        first = keep.tile([P, PACK, S], F32)
+        larger = keep.tile([P, PACK, S], F32)
         z_grouped = [keep.tile([P, half, PACK], BF16, name=f"z_grouped{u}", align_bytes=64) for u in range(2)]
         z_codes = [keep.tile([P, half], U32, name=f"z_codes{u}", align_bytes=64) for u in range(2)]
         z_scales = [keep.tile([P, half], U8, name=f"z_scales{u}", align_bytes=64) for u in range(2)]
+        halves = [slice(0, half), slice(half, S)]
+        units = [(0, slice(0, S)), (1, slice(0, S))] + [(t, cols) for cols in halves for t in (2, 3)]
+        seconds = {}
         s_banks = {}
 
-        def places(u):
-            return slice(half * u, half * (u + 1))
+        def entries(cols):
+            return slice(cols.start // 16, cols.stop // 16)
 
-        def entries(u):
-            return slice(half // 16 * u, half // 16 * (u + 1))
+        def spare(cols):
+            return slice(S + cols.start, S + cols.stop)
 
-        def gate(t, u):
+        def gate(k):
+            t, cols = units[k]
             nc.scalar.activation(
-                gates[t][:, places(u)], h_rows[t][:].indirect(n1_list[:, entries(u)]), ACT.Sigmoid
+                ex_rows[t][:, spare(cols)], rows[t][:].indirect(n1_list[:, entries(cols)]), ACT.Sigmoid
             )
 
-        def choose(t, u):
-            second = keep.tile([P, half], F32, name=f"second{t}{u}")
-            first = keep.tile([P, half], F32, name=f"first{t}{u}")
-            nc.vector.tensor_copy(second[:], h_rows[t][:].indirect(n2_list[:, entries(u)]))
-            nc.vector.tensor_tensor(first[:], h_rows[t][:, places(u)], gates[t][:, places(u)], ALU.mult)
+        def take_second(k):
+            t, cols = units[k]
+            second = keep.tile([P, S], F32, name=f"second{k}", tag="second", bufs=2)
+            seconds[k] = second[:, : cols.stop - cols.start]
+            nc.vector.tensor_copy(seconds[k], rows[t][:].indirect(n2_list[:, entries(cols)]))
+
+        def take_first(k):
+            t, cols = units[k]
             nc.vector.tensor_tensor(
-                s_rows[t][:, S + half * u : S + half * (u + 1)], first[:], second[:], ALU.max
+                first[:, t, cols], rows[t][:, cols], ex_rows[t][:, spare(cols)], ALU.mult
             )
 
-        def weigh(t, u):
-            nc.scalar.activation(
-                z_planes[u][:, t, :],
-                s_rows[t][:, S + half * u : S + half * (u + 1)],
-                ACT.Copy,
-                scale=gain[:, t : t + 1],
+        def take_larger(k):
+            t, cols = units[k]
+            nc.vector.tensor_tensor(larger[:, t, cols], first[:, t, cols], seconds[k], ALU.max)
+
+        def weigh(u):
+            nc.vector.tensor_tensor(
+                z_grouped[u][:].rearrange("p (c i) t -> p c t i", i=4),
+                larger[:, :, halves[u]].rearrange("p t (c i) -> p c t i", i=4),
+                gain[:].unsqueeze(1).unsqueeze(3).to_broadcast([P, half // 4, PACK, 4]),
+                ALU.mult,
             )
 
         def score(u):
@@ -165,52 +188,51 @@ def tile_picked_pqcgmaxlse_none_p_kernel(
                 )
                 s_banks[t, u] = bank
 
-        def exp_own(t, u):
-            nc.scalar.activation(own[t][:, places(u)], s_banks[t, u][:], ACT.Exp, scale=0.0625)
+        def exponentials(t, u):
+            nc.scalar.activation(ex_rows[t][:, halves[u]], s_banks[t, u][:], ACT.Exp, scale=0.0625)
+            nc.scalar.activation(ex_own[t][:, halves[u]], s_banks[t, u][:], ACT.Exp, scale=0.0625)
+
+        def negated(t, u):
+            nc.scalar.activation(rows[t][:, halves[u]], s_banks[t, u][:], ACT.Copy, scale=-0.0625)
 
         for t in range(PACK):
-            nc.scalar.activation(h_rows[t][:], h_banks[t][:], ACT.Copy, scale=0.0625)
-            gate(t, 0)
-        for t in range(PACK):
-            choose(t, 0)
-            gate(t, 1)
-            weigh(t, 0)
-        nc.scalar.copy(z_grouped[0][:], z_planes[0][:].rearrange("p t j -> p j t"))
-        choose(0, 1)
-        weigh(0, 1)
-        choose(1, 1)
+            nc.scalar.activation(rows[t][:, :S], h_banks[t][:], ACT.Copy, scale=0.0625)
+            gate(t)
+        gate(4)
+        gate(5)
+        take_second(0)
+        for k in range(4):
+            take_first(k)
+            take_second(k + 1)
+            take_larger(k)
+        take_first(4)
+        weigh(0)
+        take_second(5)
         score(0)
-        exp_own(0, 0)
-        weigh(1, 1)
-        choose(2, 1)
-        weigh(2, 1)
-        choose(3, 1)
-        weigh(3, 1)
-        for t in range(PACK):
-            nc.scalar.activation(s_rows[t][:, places(0)], s_banks[t, 0][:], ACT.Copy, scale=0.0625)
-        for t in range(1, PACK):
-            exp_own(t, 0)
-        nc.vector.tensor_copy(z_grouped[1][:], z_planes[1][:].rearrange("p t j -> p j t"))
+        take_first(5)
+        take_larger(4)
+        take_larger(5)
+        weigh(1)
         score(1)
 
-        sums, taken = [], []
         for t in range(PACK):
-            nc.vector.tensor_scalar_mul(s_rows[t][:, places(1)], s_banks[t, 1][:], 0.0625)
+            exponentials(t, 0)
         for t in range(PACK):
-            other = keep.tile([P, S], F32, name=f"other{t}")
+            negated(t, 0)
+        sums = []
+        for t in range(PACK):
             both = keep.tile([P, S], F32, name=f"both{t}")
-            less = keep.tile([P, S], F32, name=f"less{t}")
-            nc.scalar.activation(own[t][:, places(1)], s_rows[t][:, places(1)], ACT.Exp)
-            nc.scalar.activation(other[:], s_rows[t][:].indirect(n3_list[:]), ACT.Exp)
-            nc.vector.tensor_copy(less[:], s_rows[t][:].indirect(n4_list[:]))
-            nc.vector.tensor_tensor(both[:], own[t][:], other[:], ALU.add)
+            exponentials(t, 1)
+            nc.vector.tensor_tensor(both[:], ex_rows[t][:].indirect(n3_list[:]), ex_own[t][:], ALU.add)
             sums.append(both)
-            taken.append(less)
         out_rows = out.rearrange("(p t) j -> t p j", t=PACK)
         for t in range(PACK):
             logs = keep.tile([P, S], F32, name=f"logs{t}")
             result = keep.tile([P, S], F32, name=f"result{t}")
-            for cols in [slice(0, S)] if t < PACK - 1 else [places(0), places(1)]:
-                nc.scalar.activation(logs[:, cols], sums[t][:, cols], ACT.Ln)
-                nc.vector.tensor_tensor(result[:, cols], logs[:, cols], taken[t][:, cols], ALU.subtract)
+            negated(t, 1)
+            nc.scalar.activation(logs[:], sums[t][:], ACT.Ln)
+            for cols in [slice(0, S)] if t < PACK - 1 else halves:
+                nc.vector.tensor_tensor(
+                    result[:, cols], rows[t][:].indirect(n4_list[:, entries(cols)]), logs[:, cols], ALU.add
+                )
                 nc.sync.dma_start(out_rows[t][:, cols], result[:, cols])

@@ -37,39 +37,41 @@ def tile_picked_pqcgmaxlse_none_p_kernel(
         d_bytes = keep.tile([P, G], U8, align_bytes=64)
         x_table = keep.tile([P, T], U32, align_bytes=64)
         x_bytes = keep.tile([P, T], U8, align_bytes=64)
-        w_scales = keep.tile([P, H], U8, align_bytes=64)
+        w_bytes_placed = staging.tile([P, H], U8, align_bytes=64, offset=4 * H)
         gain = keep.tile([P, PACK], F32)
+        warm = keep.tile([P, 8], F32)
         warmed = keep.tile([P, 8], F32)
-
-        rows = [keep.tile([P, 2 * S], F32, name=f"rows{t}", align_bytes=64) for t in range(PACK)]
 
         nc.vector.memset(d_bytes[:].bitcast(I32), 0)
         nc.gpsimd.memset(x_bytes[:].bitcast(I32), 0)
-        nc.vector.memset(w_scales[:].bitcast(I32), 0)
-        for t in range(PACK):
-            nc.vector.memset(rows[t][:, S:], 0.0)
+        nc.vector.memset(w_bytes_placed[:].bitcast(I32), 0)
+        nc.vector.memset(warm[:], 0.0)
 
-        k1_list = load_list("k1_list", k1)
+        nc.sync.dma_start(
+            x_table[:].bitcast(I32), x_words[0].rearrange("p n r -> p (n r)").bitcast(I32)
+        )
         offs_list = load_list("offs_list", offs)
+        k1_list = load_list("k1_list", k1)
         nc.sync.dma_start(d_bytes[0:P:8, :].bitcast(I32), d_scales[0].bitcast(I32))
+        nc.sync.dma_start(
+            d_table[:].bitcast(I32), d_words[0].rearrange("p n r -> p (n r)").bitcast(I32)
+        )
         for q in range(4):
             nc.sync.dma_start(
                 x_bytes[32 * q : 32 * q + 4, :].bitcast(I32),
                 x_scales[0, 4 * q : 4 * q + 4, :].bitcast(I32),
             )
+        nc.sync.dma_start(gain[:], gs.rearrange("(p t) o -> p (t o)", t=PACK))
         cand_list = load_list("cand_list", cand)
         n1_list = load_list("n1_list", n1)
-        nc.sync.dma_start(
-            x_table[:].bitcast(I32), x_words[0].rearrange("p n r -> p (n r)").bitcast(I32)
-        )
         n2_list = load_list("n2_list", n2)
-        nc.sync.dma_start(
-            d_table[:].bitcast(I32), d_words[0].rearrange("p n r -> p (n r)").bitcast(I32)
-        )
-        nc.sync.dma_start(gain[:], gs.rearrange("(p t) o -> p (t o)", t=PACK))
         n3_list = load_list("n3_list", n3)
         n4_list = load_list("n4_list", n4)
-        nc.scalar.activation(warmed[:], rows[0][:, S : S + 8], ACT.Sigmoid)
+        nc.scalar.activation(warmed[:], warm[:], ACT.Sigmoid)
+        gain_size = keep.tile([P, PACK, S // 2], F32)
+        gain_sign = keep.tile([P, S // 2, PACK], BF16)
+        nc.scalar.activation(gain_size[:], gain[:].unsqueeze(2).to_broadcast([P, PACK, S // 2]), ACT.Abs)
+        nc.scalar.activation(gain_sign[:], gain[:].unsqueeze(1).to_broadcast([P, S // 2, PACK]), ACT.Sign)
 
         def gather(picked, table, offsets):
             nc.vector.tensor_copy(picked[:], table[:].indirect(offsets[:]))
@@ -81,21 +83,21 @@ def tile_picked_pqcgmaxlse_none_p_kernel(
             )
 
         w_bytes_picked = keep.tile([P, H], U8)
-        w_bytes = keep.tile([P, H], U8)
-        w_codes_picked = staging.tile([P, H], U32, offset=0)
+        w_scales = keep.tile([P, H], U8, align_bytes=64)
+        w_codes_picked = staging.tile([P, H], U32, align_bytes=64, offset=0)
         w_codes = keep.tile([P, H], U32, align_bytes=64)
         xq_codes = keep.tile([P, S], U32, align_bytes=64)
         xq_scales = keep.tile([P, S], U8, align_bytes=64)
         gather(w_bytes_picked, d_bytes, k1_list)
-        gather(xq_scales, x_bytes, offs_list)
-        deal(w_bytes, w_bytes_picked)
         for b in range(4):
             nc.sync.dma_start(
-                w_scales[b:P:32, :].bitcast(I32), w_bytes[8 * b : P : 32, :].bitcast(I32)
+                w_bytes_placed[b:P:32, :].bitcast(I32), w_bytes_picked[8 * b : P : 32, :].bitcast(I32)
             )
-        gather(w_codes_picked, d_table, k1_list)
         gather(xq_codes, x_table, offs_list)
+        gather(w_codes_picked, d_table, k1_list)
+        gather(xq_scales, x_bytes, offs_list)
         deal(w_codes, w_codes_picked)
+        deal(w_scales, w_bytes_placed)
 
         h_banks = [psum.tile([P, S], F32, name=f"h_bank{t}", tag=f"bank{t}") for t in range(PACK)]
         for t in range(PACK):
@@ -110,8 +112,8 @@ def tile_picked_pqcgmaxlse_none_p_kernel(
                 stop=True,
             )
 
-        c_scales_picked = staging.tile([P, C], U8, offset=0)
-        c_codes_picked = staging.tile([P, C], U32, offset=C)
+        c_scales_picked = staging.tile([P, C], U8, align_bytes=64, offset=4 * C + C // 2)
+        c_codes_picked = staging.tile([P, C], U32, align_bytes=64, offset=C // 2)
         c_codes = keep.tile([P, C], U32, align_bytes=64)
         c_scales = keep.tile([P, C], U8, align_bytes=64)
         gather(c_codes_picked, x_table, cand_list)
@@ -120,16 +122,16 @@ def tile_picked_pqcgmaxlse_none_p_kernel(
         deal(c_scales, c_scales_picked)
 
         half = S // 2
+        h_rows = [keep.tile([P, S], F32, name=f"h_rows{t}", align_bytes=64) for t in range(PACK)]
         ex_rows = [keep.tile([P, 2 * S], F32, name=f"ex_rows{t}", align_bytes=64) for t in range(PACK)]
-        ex_own = [keep.tile([P, S], F32, name=f"ex_own{t}") for t in range(PACK)]
+        s_rows = [keep.tile([P, 2 * S], F32, name=f"s_rows{t}", align_bytes=64) for t in range(PACK)]
         first = keep.tile([P, PACK, S], F32)
-        larger = keep.tile([P, PACK, S], F32)
+        second = keep.tile([P, PACK, S], F32)
+        z_sizes = [keep.tile([P, half, PACK], BF16, name=f"z_sizes{u}", align_bytes=64) for u in range(2)]
         z_grouped = [keep.tile([P, half, PACK], BF16, name=f"z_grouped{u}", align_bytes=64) for u in range(2)]
         z_codes = [keep.tile([P, half], U32, name=f"z_codes{u}", align_bytes=64) for u in range(2)]
         z_scales = [keep.tile([P, half], U8, name=f"z_scales{u}", align_bytes=64) for u in range(2)]
         halves = [slice(0, half), slice(half, S)]
-        units = [(0, slice(0, S)), (1, slice(0, S))] + [(t, cols) for cols in halves for t in (2, 3)]
-        seconds = {}
         s_banks = {}
 
         def entries(cols):
@@ -138,33 +140,42 @@ def tile_picked_pqcgmaxlse_none_p_kernel(
         def spare(cols):
             return slice(S + cols.start, S + cols.stop)
 
-        def gate(k):
-            t, cols = units[k]
+        def gate(t, cols):
             nc.scalar.activation(
-                ex_rows[t][:, spare(cols)], rows[t][:].indirect(n1_list[:, entries(cols)]), ACT.Sigmoid
+                ex_rows[t][:, spare(cols)], h_rows[t][:].indirect(n1_list[:, entries(cols)]), ACT.Sigmoid
             )
 
-        def take_second(k):
-            t, cols = units[k]
-            second = keep.tile([P, S], F32, name=f"second{k}", tag="second", bufs=2)
-            seconds[k] = second[:, : cols.stop - cols.start]
-            nc.vector.tensor_copy(seconds[k], rows[t][:].indirect(n2_list[:, entries(cols)]))
-
-        def take_first(k):
-            t, cols = units[k]
+        def take_second(t, cols):
             nc.vector.tensor_tensor(
-                first[:, t, cols], rows[t][:, cols], ex_rows[t][:, spare(cols)], ALU.mult
+                second[:, t, cols],
+                h_rows[t][:].indirect(n2_list[:, entries(cols)]),
+                gain_size[:, t, :],
+                ALU.mult,
             )
 
-        def take_larger(k):
-            t, cols = units[k]
-            nc.vector.tensor_tensor(larger[:, t, cols], first[:, t, cols], seconds[k], ALU.max)
+        def take_first(t, cols):
+            nc.vector.scalar_tensor_tensor(
+                first[:, t, cols],
+                h_rows[t][:, cols],
+                gain_size[:, t, 0:1],
+                ex_rows[t][:, spare(cols)],
+                ALU.mult,
+                ALU.mult,
+            )
 
-        def weigh(u):
+        def take_larger(u):
             nc.vector.tensor_tensor(
-                z_grouped[u][:].rearrange("p (c i) t -> p c t i", i=4),
-                larger[:, :, halves[u]].rearrange("p t (c i) -> p c t i", i=4),
-                gain[:].unsqueeze(1).unsqueeze(3).to_broadcast([P, half // 4, PACK, 4]),
+                z_sizes[u][:].rearrange("p (c i) t -> p c t i", i=4),
+                first[:, :, halves[u]].rearrange("p t (c i) -> p c t i", i=4),
+                second[:, :, halves[u]].rearrange("p t (c i) -> p c t i", i=4),
+                ALU.max,
+            )
+
+        def restore_sign(u):
+            nc.vector.tensor_tensor(
+                z_grouped[u][:],
+                z_sizes[u][:],
+                gain_sign[:],
                 ALU.mult,
             )
 
@@ -190,49 +201,52 @@ def tile_picked_pqcgmaxlse_none_p_kernel(
 
         def exponentials(t, u):
             nc.scalar.activation(ex_rows[t][:, halves[u]], s_banks[t, u][:], ACT.Exp, scale=0.0625)
-            nc.scalar.activation(ex_own[t][:, halves[u]], s_banks[t, u][:], ACT.Exp, scale=0.0625)
+            nc.scalar.activation(s_rows[t][:, spare(halves[u])], s_banks[t, u][:], ACT.Exp, scale=0.0625)
 
         def negated(t, u):
-            nc.scalar.activation(rows[t][:, halves[u]], s_banks[t, u][:], ACT.Copy, scale=-0.0625)
+            nc.scalar.activation(s_rows[t][:, halves[u]], s_banks[t, u][:], ACT.Copy, scale=-0.0625)
 
+        whole = slice(0, S)
         for t in range(PACK):
-            nc.scalar.activation(rows[t][:, :S], h_banks[t][:], ACT.Copy, scale=0.0625)
-            gate(t)
-        gate(4)
-        gate(5)
-        take_second(0)
-        for k in range(4):
-            take_first(k)
-            take_second(k + 1)
-            take_larger(k)
-        take_first(4)
-        weigh(0)
-        take_second(5)
+            nc.scalar.activation(h_rows[t][:], h_banks[t][:], ACT.Copy, scale=0.0625)
+            gate(t, halves[0])
+        for t in range(PACK):
+            gate(t, halves[1])
+        nc.scalar.activation(warmed[:], ex_rows[PACK - 1][:, 2 * S - 8 :], ACT.Exp)
+        for t in range(PACK):
+            take_second(t, halves[0])
+            take_first(t, halves[0])
+        take_second(0, halves[1])
+        take_larger(0)
+        take_first(0, halves[1])
+        restore_sign(0)
+        take_second(1, halves[1])
         score(0)
-        take_first(5)
-        take_larger(4)
-        take_larger(5)
-        weigh(1)
+        take_first(1, halves[1])
+        for t in range(2, PACK):
+            take_second(t, halves[1])
+            take_first(t, halves[1])
+        take_larger(1)
+        restore_sign(1)
         score(1)
 
         for t in range(PACK):
             exponentials(t, 0)
-        for t in range(PACK):
-            negated(t, 0)
         sums = []
         for t in range(PACK):
             both = keep.tile([P, S], F32, name=f"both{t}")
             exponentials(t, 1)
-            nc.vector.tensor_tensor(both[:], ex_rows[t][:].indirect(n3_list[:]), ex_own[t][:], ALU.add)
+            nc.vector.tensor_tensor(both[:], ex_rows[t][:].indirect(n3_list[:]), s_rows[t][:, S:], ALU.add)
             sums.append(both)
         out_rows = out.rearrange("(p t) j -> t p j", t=PACK)
         for t in range(PACK):
             logs = keep.tile([P, S], F32, name=f"logs{t}")
             result = keep.tile([P, S], F32, name=f"result{t}")
+            negated(t, 0)
             negated(t, 1)
             nc.scalar.activation(logs[:], sums[t][:], ACT.Ln)
-            for cols in [slice(0, S)] if t < PACK - 1 else halves:
+            for cols in [whole] if t < PACK - 1 else halves:
                 nc.vector.tensor_tensor(
-                    result[:, cols], rows[t][:].indirect(n4_list[:, entries(cols)]), logs[:, cols], ALU.add
+                    result[:, cols], s_rows[t][:].indirect(n4_list[:, entries(cols)]), logs[:, cols], ALU.add
                 )
                 nc.sync.dma_start(out_rows[t][:, cols], result[:, cols])

from contextlib import ExitStack

import concourse.mybir as mybir

K, T, S, G, H, C = 512, 1024, 512, 2048, 512, 512
P = 128
PACK = 4
FLOPS = 2 * K * H * S + 2 * K * C * S

F32 = mybir.dt.float32
BF16 = mybir.dt.bfloat16
I32 = mybir.dt.int32
U32 = mybir.dt.uint32
U16 = mybir.dt.uint16
U8 = mybir.dt.uint8
FP8X4 = mybir.dt.float8_e4m3fn_x4
ACT = mybir.ActivationFunctionType
ALU = mybir.AluOpType


def tile_picked_pqcgmaxlse_none_p_kernel(
    tc, x_words, x_scales, d_words, d_scales, gs, offs, k1, n1, n2, cand, n3, n4, out
):
    nc = tc.nc
    with ExitStack() as ctx:
        lists = ctx.enter_context(tc.tile_pool(name="lists", bufs=1))
        keep = ctx.enter_context(tc.tile_pool(name="keep", bufs=1))
        staging = ctx.enter_context(tc.tile_pool(name="staging", bufs=1))
        psum = ctx.enter_context(tc.psum_pool(name="psum", bufs=1))

        def load_list(name, source):
            tile = lists.tile([P, S // 16], U16, name=name)
            nc.sync.dma_start(tile[:], source)
            return tile

        d_table = keep.tile([P, G], U32, align_bytes=64)
        d_bytes = keep.tile([P, G], U8, align_bytes=64)
        x_table = keep.tile([P, T], U32, align_bytes=64)
        x_bytes = keep.tile([P, T], U8, align_bytes=64)
        w_bytes_placed = staging.tile([P, H], U8, align_bytes=64, offset=4 * H)
        gain = keep.tile([P, PACK], F32)
        warm = keep.tile([P, 8], F32)
        warmed = keep.tile([P, 8], F32)

        nc.vector.memset(d_bytes[:].bitcast(I32), 0)
        nc.gpsimd.memset(x_bytes[:].bitcast(I32), 0)
        nc.vector.memset(w_bytes_placed[:].bitcast(I32), 0)
        nc.vector.memset(warm[:], 0.0)

        nc.sync.dma_start(
            x_table[:].bitcast(I32), x_words[0].rearrange("p n r -> p (n r)").bitcast(I32)
        )
        offs_list = load_list("offs_list", offs)
        k1_list = load_list("k1_list", k1)
        nc.sync.dma_start(d_bytes[0:P:8, :].bitcast(I32), d_scales[0].bitcast(I32))
        nc.sync.dma_start(
            d_table[:].bitcast(I32), d_words[0].rearrange("p n r -> p (n r)").bitcast(I32)
        )
        for q in range(4):
            nc.sync.dma_start(
                x_bytes[32 * q : 32 * q + 4, :].bitcast(I32),
                x_scales[0, 4 * q : 4 * q + 4, :].bitcast(I32),
            )
        nc.sync.dma_start(gain[:], gs.rearrange("(p t) o -> p (t o)", t=PACK))
        cand_list = load_list("cand_list", cand)
        n1_list = load_list("n1_list", n1)
        n2_list = load_list("n2_list", n2)
        n3_list = load_list("n3_list", n3)
        n4_list = load_list("n4_list", n4)
        nc.scalar.activation(warmed[:], warm[:], ACT.Sigmoid)
        gain_size = keep.tile([P, PACK, S // 2], F32)
        gain_sign = keep.tile([P, S // 2, PACK], BF16)
        nc.scalar.activation(gain_size[:], gain[:].unsqueeze(2).to_broadcast([P, PACK, S // 2]), ACT.Abs)
        nc.scalar.activation(gain_sign[:], gain[:].unsqueeze(1).to_broadcast([P, S // 2, PACK]), ACT.Sign)

        def gather(picked, table, offsets):
            nc.vector.tensor_copy(picked[:], table[:].indirect(offsets[:]))

        def deal(dealt, picked):
            nc.vector.tensor_copy(
                dealt[:].rearrange("p (t m) -> p t m", t=PACK),
                picked[:].rearrange("p (m t) -> p t m", t=PACK),
            )

        w_bytes_picked = keep.tile([P, H], U8)
        w_scales = keep.tile([P, H], U8, align_bytes=64)
        w_codes_picked = staging.tile([P, H], U32, align_bytes=64, offset=0)
        w_codes = keep.tile([P, H], U32, align_bytes=64)
        xq_codes = keep.tile([P, S], U32, align_bytes=64)
        xq_scales = keep.tile([P, S], U8, align_bytes=64)
        gather(w_bytes_picked, d_bytes, k1_list)
        for b in range(4):
            nc.sync.dma_start(
                w_bytes_placed[b:P:32, :].bitcast(I32), w_bytes_picked[8 * b : P : 32, :].bitcast(I32)
            )
        gather(xq_codes, x_table, offs_list)
        gather(w_codes_picked, d_table, k1_list)
        gather(xq_scales, x_bytes, offs_list)
        deal(w_codes, w_codes_picked)
        deal(w_scales, w_bytes_placed)

        h_banks = [psum.tile([P, S], F32, name=f"h_bank{t}", tag=f"bank{t}") for t in range(PACK)]
        for t in range(PACK):
            cols = slice(P * t, P * (t + 1))
            nc.tensor.matmul_mx(
                out=h_banks[t][:],
                lhsT=w_codes[:, cols].bitcast(FP8X4),
                lhsT_scale=w_scales[:, cols],
                rhs=xq_codes[:].bitcast(FP8X4),
                rhs_scale=xq_scales[:],
                start=True,
                stop=True,
            )

        c_scales_picked = staging.tile([P, C], U8, align_bytes=64, offset=4 * C + C // 2)
        c_codes_picked = staging.tile([P, C], U32, align_bytes=64, offset=C // 2)
        c_codes = keep.tile([P, C], U32, align_bytes=64)
        c_scales = keep.tile([P, C], U8, align_bytes=64)
        gather(c_codes_picked, x_table, cand_list)
        gather(c_scales_picked, x_bytes, cand_list)
        deal(c_codes, c_codes_picked)
        deal(c_scales, c_scales_picked)

        half = S // 2
        h_rows = [keep.tile([P, S], F32, name=f"h_rows{t}", align_bytes=64) for t in range(PACK)]
        ex_rows = [keep.tile([P, 2 * S], F32, name=f"ex_rows{t}", align_bytes=64) for t in range(PACK)]
        s_rows = [keep.tile([P, 2 * S], F32, name=f"s_rows{t}", align_bytes=64) for t in range(PACK)]
        first = keep.tile([P, PACK, S], F32)
        second = keep.tile([P, PACK, S], F32)
        z_sizes = [keep.tile([P, half, PACK], BF16, name=f"z_sizes{u}", align_bytes=64) for u in range(2)]
        z_grouped = [keep.tile([P, half, PACK], BF16, name=f"z_grouped{u}", align_bytes=64) for u in range(2)]
        z_codes = [keep.tile([P, half], U32, name=f"z_codes{u}", align_bytes=64) for u in range(2)]
        z_scales = [keep.tile([P, half], U8, name=f"z_scales{u}", align_bytes=64) for u in range(2)]
        halves = [slice(0, half), slice(half, S)]
        s_banks = {}

        def entries(cols):
            return slice(cols.start // 16, cols.stop // 16)

        def spare(cols):
            return slice(S + cols.start, S + cols.stop)

        def gate(t, cols):
            nc.scalar.activation(
                ex_rows[t][:, spare(cols)], h_rows[t][:].indirect(n1_list[:, entries(cols)]), ACT.Sigmoid
            )

        def take_second(t, cols):
            nc.vector.tensor_tensor(
                second[:, t, cols],
                h_rows[t][:].indirect(n2_list[:, entries(cols)]),
                gain_size[:, t, :],
                ALU.mult,
            )

        def take_first(t, cols):
            nc.vector.scalar_tensor_tensor(
                first[:, t, cols],
                h_rows[t][:, cols],
                gain_size[:, t, 0:1],
                ex_rows[t][:, spare(cols)],
                ALU.mult,
                ALU.mult,
            )

        def take_larger(u):
            nc.vector.tensor_tensor(
                z_sizes[u][:].rearrange("p (c i) t -> p c t i", i=4),
                first[:, :, halves[u]].rearrange("p t (c i) -> p c t i", i=4),
                second[:, :, halves[u]].rearrange("p t (c i) -> p c t i", i=4),
                ALU.max,
            )

        def restore_sign(u):
            nc.vector.tensor_tensor(
                z_grouped[u][:],
                z_sizes[u][:],
                gain_sign[:],
                ALU.mult,
            )

        def score(u):
            nc.vector.quantize_mx(
                out=z_codes[u][:].bitcast(FP8X4),
                scales=z_scales[u][:],
                in_=z_grouped[u][:].rearrange("p j t -> p (j t)"),
            )
            for t in range(PACK):
                cols = slice(P * t, P * (t + 1))
                bank = psum.tile([P, half], F32, name=f"s_bank{t}{u}", tag=f"bank{t + PACK * (1 - u)}")
                nc.tensor.matmul_mx(
                    out=bank[:],
                    lhsT=c_codes[:, cols].bitcast(FP8X4),
                    lhsT_scale=c_scales[:, cols],
                    rhs=z_codes[u][:].bitcast(FP8X4),
                    rhs_scale=z_scales[u][:],
                    start=True,
                    stop=True,
                )
                s_banks[t, u] = bank

        def exponentials(t, u):
            nc.scalar.activation(ex_rows[t][:, halves[u]], s_banks[t, u][:], ACT.Exp, scale=0.0625)
            nc.scalar.activation(s_rows[t][:, spare(halves[u])], s_banks[t, u][:], ACT.Exp, scale=0.0625)

        def negated(t, u):
            nc.scalar.activation(s_rows[t][:, halves[u]], s_banks[t, u][:], ACT.Copy, scale=-0.0625)

        whole = slice(0, S)
        for t in range(PACK):
            nc.scalar.activation(h_rows[t][:], h_banks[t][:], ACT.Copy, scale=0.0625)
            gate(t, halves[0])
        for t in range(PACK):
            gate(t, halves[1])
        nc.scalar.activation(warmed[:], ex_rows[PACK - 1][:, 2 * S - 8 :], ACT.Exp)
        for t in range(PACK):
            take_second(t, halves[0])
            take_first(t, halves[0])
        take_second(0, halves[1])
        take_larger(0)
        take_first(0, halves[1])
        restore_sign(0)
        take_second(1, halves[1])
        score(0)
        take_first(1, halves[1])
        for t in range(2, PACK):
            take_second(t, halves[1])
            take_first(t, halves[1])
        take_larger(1)
        restore_sign(1)
        score(1)

        for t in range(PACK):
            exponentials(t, 0)
        sums = []
        for t in range(PACK):
            both = keep.tile([P, S], F32, name=f"both{t}")
            exponentials(t, 1)
            nc.vector.tensor_tensor(both[:], ex_rows[t][:].indirect(n3_list[:]), s_rows[t][:, S:], ALU.add)
            sums.append(both)
        out_rows = out.rearrange("(p t) j -> t p j", t=PACK)
        for t in range(PACK):
            logs = keep.tile([P, S], F32, name=f"logs{t}")
            result = keep.tile([P, S], F32, name=f"result{t}")
            negated(t, 0)
            negated(t, 1)
            nc.scalar.activation(logs[:], sums[t][:], ACT.Ln)
            for cols in [whole] if t < PACK - 1 else halves:
                nc.vector.tensor_tensor(
                    result[:, cols], s_rows[t][:].indirect(n4_list[:, entries(cols)]), logs[:, cols], ALU.add
                )
                nc.sync.dma_start(out_rows[t][:, cols], result[:, cols])
